import numpy as np
import ml_dtypes


def mxq(x, axis, fmt="e4m3"):
    dtype, down = {"e4m3": (ml_dtypes.float8_e4m3fn, 7), "e5m2": (ml_dtypes.float8_e5m2, 14)}[fmt]
    v = np.moveaxis(np.asarray(x, np.float32).astype(ml_dtypes.bfloat16).astype(np.float64), axis, -1)
    blocks = v.reshape(v.shape[:-1] + (-1, 32))
    amax = np.abs(blocks).max(-1, keepdims=True)
    byte = np.maximum(np.where(amax > 0, np.frexp(amax)[1] - 1 + 127, 0) - down, 1)
    scale = np.exp2(byte - 127.0)
    codes = (blocks / scale).astype(np.float32).astype(dtype).astype(np.float64)
    return np.moveaxis((codes * scale).reshape(v.shape), -1, axis)


WIDE = False


def mx_kscale(k):
    if not WIDE:
        return np.ones(k)
    levels = np.array([10, -10, 5, -5, 0])
    if k % 512:
        return np.exp2(np.random.permutation(np.resize(levels, k // 32))).repeat(32)
    a = np.empty((k // 512, 16))
    for p in range(k // 512):
        a[p, :8] = np.random.permutation(np.resize(levels, 8))
        for g in range(8):
            far = levels[np.abs(levels - a[p, g]) >= 10]
            a[p, g + 8] = far[np.random.randint(len(far))]
    return np.exp2(a.ravel()).repeat(32)


def f64(x):
    return np.asarray(x).astype(np.float64)


def striped(idx):
    return np.tile(idx.reshape(-1, 16).T, (8, 1)).astype(np.uint16)


def unstriped(offs):
    return offs[:16].T.reshape(-1).astype(np.int64)


E2M1 = np.array([0.0, 0.5, 1.0, 1.5, 2.0, 3.0, 4.0, 6.0, -0.0, -0.5, -1.0, -1.5, -2.0, -3.0, -4.0, -6.0])


def pack_weight(w, fmt):
    k, n = w.shape
    w = f64(np.asarray(w, np.float32).astype(ml_dtypes.bfloat16)).reshape(k // 32, 32, n)
    amax = np.abs(w).max(1)
    if fmt == "e4m3":
        byte = np.frexp(amax)[1] - 1 + 127 - 7
    else:
        mant, ex = np.frexp(amax / 6.0)
        byte = np.where(mant > 0.5, ex, ex - 1) + 127
    byte = np.clip(np.where(amax > 0, byte, 1), 1, 254)
    scaled = (w * np.exp2(127.0 - byte)[:, None, :]).reshape(k, n).astype(np.float32)
    by_word = np.ascontiguousarray(scaled.reshape(k // 512, 128, 4, n).transpose(0, 1, 3, 2))
    if fmt == "e4m3":
        words = by_word.astype(ml_dtypes.float8_e4m3fn).view(np.uint8)
    else:
        c = by_word.astype(ml_dtypes.float4_e2m1fn).view(np.uint8) & 0xF
        words = (c[..., 0::2] | (c[..., 1::2] << 4)).reshape(k // 512, 128, 2 * n)
    return np.ascontiguousarray(words), np.ascontiguousarray(byte.astype(np.uint8).reshape(k // 512, 16, n))


def unpack_weight(words, scales, fmt):
    g, _, n = scales.shape
    words = np.ascontiguousarray(words).reshape(g, 128, n, -1)
    if fmt == "e4m3":
        vals = words.view(ml_dtypes.float8_e4m3fn).astype(np.float64)
    else:
        nib = np.empty((g, 128, n, 4), np.uint8)
        nib[..., 0::2] = words & 0xF
        nib[..., 1::2] = words >> 4
        vals = E2M1[nib]
    vals = vals * np.repeat(np.exp2(scales.astype(np.float64) - 127.0), 8, axis=1)[..., None]
    return vals.transpose(0, 1, 3, 2).reshape(g * 512, n)


def gelu(v):
    return 0.5 * v * (1.0 + np.tanh(np.sqrt(2.0 / np.pi) * (v + 0.044715 * v**3)))


K1, K2, H, N, T, S, T2 = 1024, 1536, 512, 768, 2048, 512, 1024

def setup_inputs():
    n = np.random.standard_normal
    s1 = mx_kscale(K1)[:, None]
    s2 = mx_kscale(K2)[:, None]
    u = mx_kscale(2 * H)[:, None]
    tab_words, tab_scales = pack_weight(n((K1, T)) * s1, "e4m3")
    tab2_words, tab2_scales = pack_weight(n((K2, T)) * s2, "e4m3")
    w2_words, w2_scales = pack_weight(n((K2, H)) / np.sqrt(K2) / s2, "e2m1")
    w3_words, w3_scales = pack_weight(n((H, N)) / np.sqrt(H) / u[:H], "e4m3")
    return {
        "tab_words": tab_words, "tab_scales": tab_scales,
        "tab2_words": tab2_words, "tab2_scales": tab2_scales,
        "offs": striped(np.random.permutation(T)[:S]),
        "offs2": striped(np.random.permutation(T)[:S]),
        "offs3": striped(np.random.permutation(T2)[:S]),
        "offs4": striped(np.random.permutation(T2)[:S]),
        "w1": (1.5 * n((K1, H)) / np.sqrt(K1) / s1).astype(np.float32),
        "w2_words": w2_words, "w2_scales": w2_scales,
        "w3_words": w3_words, "w3_scales": w3_scales,
        "w4": (1.5 * n((H, N)) / np.sqrt(H) / u[H:]).astype(np.float32),
        "delay": np.exp(0.3 * n(H)).astype(np.float32),
        "gain": (np.exp(0.3 * n(2 * H)) * u[:, 0]).astype(np.float32),
        "elev": (0.8 * n((H, T2))).astype(np.float32),
        "wg1": np.exp(0.3 * n((128, S))).astype(np.float32),
        "wg2": np.exp(0.3 * n((128, S))).astype(np.float32),
    }

def reference(tab_words, tab_scales, tab2_words, tab2_scales, offs, offs2, offs3, offs4, w1, w2_words, w2_scales, w3_words, w3_scales, w4, delay, gain, elev, wg1, wg2):
    v = unpack_weight(tab_words, tab_scales, "e4m3")[:, unstriped(offs)]
    v2 = unpack_weight(tab2_words, tab2_scales, "e4m3")[:, unstriped(offs2)]
    h1 = np.tanh(mxq(f64(w1), 0, "e4m3").T @ v)
    h2 = f64(delay)[:, None] * (unpack_weight(w2_words, w2_scales, "e2m1").T @ v2)
    pa = np.zeros((H, T2))
    pa[:, unstriped(offs3)] = np.tile(f64(wg1), (H // 128, 1)) * h1
    pb = np.zeros((H, T2))
    pb[:, unstriped(offs4)] = np.tile(f64(wg2), (H // 128, 1)) * h2
    e = f64(elev)
    z = (pa + e) * (pb + e)
    zq = mxq(f64(gain)[:, None] * np.concatenate([z, np.tanh(z)]), 0, "e4m3")
    w3 = unpack_weight(w3_words, w3_scales, "e4m3")
    return w3.T @ zq[:H] + mxq(f64(w4), 0, "e4m3").T @ zq[H:]

@@ -1,0 +1,359 @@
+from contextlib import ExitStack
+
+import concourse.mybir as mybir
+from concourse.masks import make_identity
+
+K1, K2, H, N, T, S, T2 = 1024, 1536, 512, 768, 2048, 512, 1024
+FLOPS = 2 * (K1 * H * S + K2 * H * S + 2 * H * N * T2)
+
+F32 = mybir.dt.float32
+BF16 = mybir.dt.bfloat16
+I32 = mybir.dt.int32
+U32 = mybir.dt.uint32
+U16 = mybir.dt.uint16
+U8 = mybir.dt.uint8
+FP8X4 = mybir.dt.float8_e4m3fn_x4
+FP4X4 = mybir.dt.float4_e2m1fn_x4
+MULT = mybir.AluOpType.mult
+COPY = mybir.ActivationFunctionType.Copy
+TANH = mybir.ActivationFunctionType.Tanh
+
+P = 128
+PACK = 4
+K_PASS = P * PACK
+QUADS = 4
+BANK = 512
+HALVES = T2 // BANK
+CHUNK = 256
+ALIGN = 64
+
+
+def tile_list_flank_unrest_score_kernel(
+    tc, tab_words, tab_scales, tab2_words, tab2_scales, offs, offs2, offs3, offs4,
+    w1, w2_words, w2_scales, w3_words, w3_scales, w4, delay, gain, elev, wg1, wg2, out,
+):
+    nc = tc.nc
+    passes1 = K1 // K_PASS
+    passes2 = K2 // K_PASS
+
+    with ExitStack() as ctx:
+        lists = ctx.enter_context(tc.tile_pool(name="lists", bufs=1))
+        sb = ctx.enter_context(tc.tile_pool(name="sb", bufs=1))
+        psum = ctx.enter_context(tc.psum_pool(name="psum", bufs=1))
+
+        def tile(shape, dtype, name, tag=None, bufs=1):
+            return sb.tile(shape, dtype, name=name, tag=tag or name, bufs=bufs, align_bytes=ALIGN)
+
+        def bank(b, name):
+            return psum.tile([P, BANK], F32, name=name, tag="bank%d" % b)
+
+        idx = lists.tile([P, S // 16], U16, name="idx")
+        idx2 = lists.tile([P, S // 16], U16, name="idx2")
+        idx3 = lists.tile([P, S // 16], U16, name="idx3")
+        idx4 = lists.tile([P, S // 16], U16, name="idx4")
+
+        tab_sc = tile([P, T], U8, "tab_sc")
+        tab2_sc = tile([P, T], U8, "tab2_sc")
+        w2_sc_raw = tile([P, passes2, H], U8, "w2_sc_raw")
+        v2_sc_moved = tile([P, passes2 - 1, S], U8, "v2_sc_moved")
+        w3_sc = tile([P, N], U8, "w3_sc")
+        nc.vector.memset(tab_sc[:].bitcast(I32), 0)
+        nc.vector.memset(tab2_sc[:].bitcast(I32), 0)
+        nc.vector.memset(w2_sc_raw[:].bitcast(I32), 0)
+        nc.vector.memset(w3_sc[:].bitcast(I32), 0)
+        nc.vector.memset(v2_sc_moved[:].bitcast(I32), 0)
+        page_a = [tile([P, T2], F32, "page_a%d" % i) for i in range(2)]
+        page_b = [tile([P, T2], F32, "page_b%d" % i) for i in range(2)]
+        for page in page_a + page_b:
+            nc.vector.memset(page[:], 0.0)
+
+        w1_raw = [tile([P, PACK, H], F32, "w1_raw%d" % a) for a in range(passes1)]
+        tab = [tile([P, T], I32, "tab_%d" % a) for a in range(passes1)]
+        tab2 = [tile([P, T], I32, "tab2_%d" % a) for a in range(passes2)]
+        w2_raw = tile([P, passes2, 2 * H], U8, "w2_raw")
+        w3 = tile([P, N], I32, "w3")
+        w4_raw = tile([P, PACK, N], F32, "w4_raw")
+        e_pair = [tile([P, 2, T2], F32, "e_pair%d" % u) for u in range(2)]
+        e = [e_pair[t // 2][:, t % 2, :] for t in range(PACK)]
+        g1_first = tile([P, 2, S], F32, "g1_first")
+        g1_third = tile([P, 1, S], F32, "g1_third")
+        g2_all = tile([P, PACK, S], F32, "g2_all")
+        g1 = {0: g1_first[:, 0, :], 1: g1_first[:, 1, :], 2: g1_third[:, 0, :]}
+        g2 = [g2_all[:, t, :] for t in range(PACK)]
+        delay_sb = tile([P, PACK], F32, "delay_sb")
+        gain_sb = tile([P, 2, PACK], F32, "gain_sb")
+
+        def load_w1(a):
+            rows = w1[a * K_PASS : (a + 1) * K_PASS, :]
+            nc.sync.dma_start(out=w1_raw[a][:], in_=rows.rearrange("(p j) c -> p j c", j=PACK))
+
+        def load_words(dst, words):
+            nc.sync.dma_start(out=dst[:], in_=words.rearrange("p n i -> p (n i)").bitcast(I32))
+
+        def load_e(u):
+            nc.sync.dma_start(out=e_pair[u][:], in_=elev.rearrange("(p t) m -> p t m", t=PACK)[:, 2 * u : 2 * u + 2, :])
+
+        def load_wg(dst, wg, t0, t1):
+            rows = wg.rearrange("(q t) j -> q (t j)", t=PACK)[:, t0 * S : t1 * S]
+            nc.sync.dma_start(
+                out=dst[:].rearrange("p t j -> p (t j)"),
+                in_=rows.unsqueeze(0).to_broadcast([QUADS, P // QUADS, (t1 - t0) * S]),
+            )
+
+        def load_packed_scales(engine, dst, scales):
+            passes = scales.shape[0]
+            for q in range(QUADS):
+                engine.dma_start(
+                    out=dst[32 * q : 32 * q + 4 * passes, :].bitcast(I32),
+                    in_=scales[:, 4 * q : 4 * q + 4, :].bitcast(I32),
+                )
+
+        def load_side_scales(engine, dst, scales):
+            for q in range(QUADS):
+                engine.dma_start(
+                    out=dst[32 * q : 32 * q + 4].bitcast(I32),
+                    in_=scales[:, 4 * q : 4 * q + 4, :].rearrange("a r c -> r a c").bitcast(I32),
+                )
+
+        nc.sync.dma_start(idx[:], offs)
+        load_w1(0)
+        load_packed_scales(nc.sync, tab_sc, tab_scales)
+        load_w1(1)
+        load_words(tab[0], tab_words[0])
+        nc.sync.dma_start(idx2[:], offs2)
+        load_packed_scales(nc.sync, tab2_sc, tab2_scales)
+        load_words(tab[1], tab_words[1])
+        nc.sync.dma_start(out=w2_raw[:].bitcast(I32), in_=w2_words.rearrange("a p c -> p a c").bitcast(I32))
+        nc.sync.dma_start(idx3[:], offs3)
+        load_wg(g1_first, wg1, 0, 2)
+        load_side_scales(nc.sync, w2_sc_raw, w2_scales)
+        load_e(0)
+        v_sc = tile([P, S], U8, "v_sc")
+        v2_sc = tile([P, S], U8, "v2_sc")
+        nc.vector.tensor_copy(v_sc[:], tab_sc[:].indirect(idx[:]))
+
+        def move_plane(a):
+            for q in range(QUADS):
+                nc.sync.dma_start(
+                    out=v2_sc_moved[32 * q : 32 * q + 4, a - 1, :].bitcast(I32),
+                    in_=v2_sc[32 * q + 4 * a : 32 * q + 4 * a + 4, :].bitcast(I32),
+                )
+
+        ident = tile([P, P], F32, "ident")
+        make_identity(nc, ident[:])
+
+        w1_codes = tile([P, passes1, H], U32, "w1_codes")
+        w1_sc = tile([P, passes1, H], U8, "w1_sc")
+        w1_bf = [tile([P, PACK * H], BF16, "w1_bf%d" % a) for a in range(passes1)]
+        v = [tile([P, S], U32, "v_%d" % a) for a in range(passes1)]
+        v2 = [tile([P, S], U32, "v2_%d" % a) for a in range(passes2)]
+
+        def gather_words(dst, table, offsets):
+            nc.vector.tensor_copy(dst[:], table[:].bitcast(U32).indirect(offsets[:]))
+
+        for a in range(passes1):
+            nc.scalar.copy(
+                out=w1_bf[a][:].rearrange("p (t m j) -> p m j t", t=PACK, j=PACK),
+                in_=w1_raw[a][:].rearrange("p j (m t) -> p m j t", t=PACK),
+            )
+        nc.vector.quantize_mx(out=w1_codes[:, 0, :].bitcast(FP8X4), scales=w1_sc[:, 0, :], in_=w1_bf[0][:])
+
+        gather_words(v[0], tab[0], idx)
+        nc.vector.quantize_mx(out=w1_codes[:, 1, :].bitcast(FP8X4), scales=w1_sc[:, 1, :], in_=w1_bf[1][:])
+        nc.vector.tensor_copy(v2_sc[:], tab2_sc[:].indirect(idx2[:]))
+        gather_words(v[1], tab[1], idx)
+        w2_dealt = tile([P, passes2, 2 * H], U8, "w2_dealt")
+        w2_sc = tile([P, passes2, H], U8, "w2_sc")
+        nc.vector.tensor_copy(
+            out=w2_dealt[:].bitcast(U16).rearrange("p a (t m) -> p a m t", t=PACK),
+            in_=w2_raw[:].bitcast(U16).rearrange("p a (m t) -> p a m t", t=PACK),
+        )
+        nc.vector.tensor_copy(
+            out=w2_sc[:].rearrange("p a (t m) -> p a m t", t=PACK),
+            in_=w2_sc_raw[:].rearrange("p a (m t) -> p a m t", t=PACK),
+        )
+
+        load_words(tab2[0], tab2_words[0])
+        load_words(tab2[1], tab2_words[1])
+        move_plane(1)
+        load_words(tab2[2], tab2_words[2])
+        move_plane(2)
+        load_wg(g1_third, wg1, 2, 3)
+        load_wg(g2_all, wg2, 0, PACK)
+        nc.sync.dma_start(out=delay_sb[:], in_=delay.rearrange("(p t) -> p t", t=PACK))
+        nc.sync.dma_start(idx4[:], offs4)
+
+        h1_ps = [bank(t, "h1_ps%d" % t) for t in range(PACK)]
+        for a in range(passes1):
+            for t in range(PACK):
+                cols = slice(t * P, (t + 1) * P)
+                nc.tensor.matmul_mx(
+                    out=h1_ps[t][:],
+                    lhsT=w1_codes[:, a, cols].bitcast(FP8X4), lhsT_scale=w1_sc[:, a, cols],
+                    rhs=v[a][:].bitcast(FP8X4), rhs_scale=v_sc[4 * a : P, :],
+                    start=(a == 0), stop=(a == passes1 - 1),
+                )
+        h1 = [tile([P, S], F32, "h1_%d" % t) for t in range(PACK)]
+        h2 = [tile([P, S], F32, "h2_%d" % t) for t in range(PACK)]
+        for t in range(PACK):
+            nc.scalar.activation(out=h1[t][:], in_=h1_ps[t][:], func=TANH)
+
+        def scatter(page, offsets, h, wg):
+            nc.vector.tensor_tensor(page[:].indirect(offsets[:]), h[:], wg, MULT)
+
+        def turned_sum(page, t, banks, name):
+            sums = [bank(b, "%s_%d" % (name, i)) for i, b in enumerate(banks)]
+            for term, src in enumerate((e[t], page)):
+                for half in range(HALVES):
+                    for j in range(BANK // P):
+                        m0 = half * BANK + j * P
+                        nc.tensor.matmul(
+                            out=sums[half][:, j * P : (j + 1) * P], lhsT=src[:, m0 : m0 + P], rhs=ident[:],
+                            is_transpose=True,
+                            start=(term == 0 and j == 0), stop=(term == 1 and j == BANK // P - 1),
+                        )
+            return sums
+
+        held_tags = ["w1_raw0", "w1_raw1", "w1_bf0", "w1_bf1"]
+
+        def hold(sums, t):
+            held = tile([P, HALVES, BANK], F32, "held%d" % t, tag=held_tags[t])
+            for half in range(HALVES):
+                nc.scalar.copy(out=held[:, half, :], in_=sums[half][:])
+            return held
+
+        zs_planes = [tile([P, PACK, BANK], BF16, "zs_planes%d" % i) for i in range(HALVES)]
+        zt_planes = [tile([P, PACK, BANK], BF16, "zt_planes%d" % i) for i in range(HALVES)]
+
+        def product(sums, held, t, banks):
+            for half in range(HALVES):
+                z_turned = tile([P, BANK], F32, "z_turned%d" % half)
+                nc.vector.tensor_tensor(z_turned[:], sums[half][:], held[:, half, :], MULT)
+                z = bank(banks[half], "z%d_%d" % (t, half))
+                for j in range(BANK // P):
+                    nc.tensor.transpose(z[:, j * P : (j + 1) * P], z_turned[:, j * P : (j + 1) * P], ident[:])
+                tag = "w4_raw" if (t, half) == (0, 0) else "tanh_z%d" % half
+                tanh_z = tile([P, BANK], F32, "tanh_z%d" % half, tag=tag)
+                nc.scalar.activation(out=zs_planes[half][:, t, :], in_=z[:], func=COPY, scale=gain_sb[:, 0, t : t + 1])
+                nc.scalar.activation(out=tanh_z[:], in_=z[:], func=TANH)
+                nc.scalar.activation(
+                    out=zt_planes[half][:, t, :], in_=tanh_z[:], func=COPY, scale=gain_sb[:, 1, t : t + 1]
+                )
+
+        held = {}
+        for t in range(2):
+            scatter(page_a[t], idx3, h1[t], g1[t])
+            held[t] = hold(turned_sum(page_a[t], t, (4 + 2 * t, 5 + 2 * t), "a%d" % t), t)
+
+        for a in range(passes2):
+            gather_words(v2[a], tab2[a], idx2)
+        load_e(1)
+        nc.sync.dma_start(out=w4_raw[:], in_=w4.rearrange("(p j) c -> p j c", j=PACK))
+        nc.sync.dma_start(out=gain_sb[:], in_=gain.rearrange("(s p t) -> p s t", s=2, t=PACK))
+        load_words(w3, w3_words[0])
+        for q in range(QUADS):
+            nc.sync.dma_start(
+                out=w3_sc[32 * q : 32 * q + 4, :].bitcast(I32),
+                in_=w3_scales[0, 4 * q : 4 * q + 4, :].bitcast(I32),
+            )
+        h2_ps = [bank(t, "h2_ps%d" % t) for t in range(PACK)]
+        for t in range(PACK):
+            cols = slice(t * P, (t + 1) * P)
+            for a in range(passes2):
+                nc.tensor.matmul_mx(
+                    out=h2_ps[t][:],
+                    lhsT=w2_dealt[:, a, 2 * t * P : 2 * (t + 1) * P].bitcast(FP4X4), lhsT_scale=w2_sc[:, a, cols],
+                    rhs=v2[a][:].bitcast(FP8X4),
+                    rhs_scale=v2_sc[:] if a == 0 else v2_sc_moved[:, a - 1, :],
+                    start=(a == 0), stop=(a == passes2 - 1),
+                )
+            nc.scalar.activation(out=h2[t][:], in_=h2_ps[t][:], func=COPY, scale=delay_sb[:, t : t + 1])
+
+        scatter(page_a[0], idx3, h1[2], g1[2])
+        held[2] = hold(turned_sum(page_a[0], 2, (4, 5), "a2"), 2)
+
+        scatter(page_b[0], idx4, h2[0], g2[0])
+        sums_b0 = turned_sum(page_b[0], 0, (6, 7), "b0")
+        w4_bf = tile([P, PACK * N], BF16, "w4_bf", tag="h2_0")
+        nc.scalar.copy(
+            out=w4_bf[:].rearrange("p (c i j) -> p c j i", i=4, j=PACK),
+            in_=w4_raw[:].rearrange("p j (c i) -> p c j i", i=4),
+        )
+        scatter(page_b[1], idx4, h2[1], g2[1])
+        sums_b1 = turned_sum(page_b[1], 1, (0, 1), "b1")
+        product(sums_b0, held[0], 0, (2, 3))
+        scatter(page_b[0], idx4, h2[2], g2[2])
+        sums_b2 = turned_sum(page_b[0], 2, (4, 5), "b2")
+        product(sums_b1, held[1], 1, (6, 7))
+        g1_last = tile([P, 1, S], F32, "g1_last", tag=held_tags[1])
+        load_wg(g1_last, wg1, 3, 4)
+        g1[3] = g1_last[:, 0, :]
+        w4_codes = tile([P, N], U32, "w4_codes", tag=held_tags[0])
+        w4_sc = tile([P, N], U8, "w4_sc")
+        for c0, c1 in ((0, 512), (512, N)):
+            nc.vector.quantize_mx(
+                out=w4_codes[:, c0:c1].bitcast(FP8X4), scales=w4_sc[:, c0:c1], in_=w4_bf[:, PACK * c0 : PACK * c1]
+            )
+        scatter(page_b[1], idx4, h2[3], g2[3])
+        held[3] = hold(turned_sum(page_b[1], 3, (0, 1), "b3"), 3)
+        product(sums_b2, held[2], 2, (2, 3))
+        scatter(page_a[1], idx3, h1[3], g1[3])
+        sums_a3 = turned_sum(page_a[1], 3, (4, 5), "a3")
+        product(sums_a3, held[3], 3, (6, 7))
+
+        chunks = T2 // CHUNK
+        pairs = N // (2 * P)
+        staged = [
+            tile([P, width, BANK], F32, "staged_" + tag, tag=tag)
+            for tag, width in (("e_pair0", 4), ("w4_raw", 6), ("g2_all", 2))
+        ]
+        slots = [st[:, i, :] for st in staged for i in range(st.shape[1])]
+        woven = {}
+
+        def weave(c, s):
+            if s == 0:
+                woven[c] = tile([P, 2, PACK * CHUNK], BF16, "woven", bufs=2)
+            planes = (zs_planes, zt_planes)[s][c * CHUNK // BANK]
+            m0 = c * CHUNK % BANK
+            nc.vector.tensor_copy(
+                out=woven[c][:, s, :].rearrange("p (c i t) -> p c t i", i=4, t=PACK),
+                in_=planes[:, :, m0 : m0 + CHUNK].rearrange("p t (c i) -> p c t i", i=4),
+            )
+
+        def score(c):
+            codes = tile([P, 2, CHUNK], U32, "z_codes", bufs=2)
+            scales = tile([P, 2, CHUNK], U8, "z_sc", bufs=2)
+            nc.vector.quantize_mx(
+                out=codes[:].rearrange("p s m -> p (s m)").bitcast(FP8X4),
+                scales=scales[:].rearrange("p s m -> p (s m)"),
+                in_=woven[c][:].rearrange("p s x -> p (s x)"),
+            )
+            for i in range(pairs):
+                acc = bank((pairs * c + i) % 8, "acc%d_%d" % (c, i))
+                for u in range(2):
+                    cols = slice((2 * i + u) * P, (2 * i + u + 1) * P)
+                    for s, (w_codes, w_sc) in enumerate(((w3, w3_sc), (w4_codes, w4_sc))):
+                        nc.tensor.matmul_mx(
+                            out=acc[:, u * CHUNK : (u + 1) * CHUNK],
+                            lhsT=w_codes[:, cols].bitcast(FP8X4), lhsT_scale=w_sc[:, cols],
+                            rhs=codes[:, s, :].bitcast(FP8X4), rhs_scale=scales[:, s, :],
+                            start=(s == 0), stop=(s == 1),
+                        )
+                slot = slots[pairs * c + i]
+                if c == chunks - 1 and i != 1:
+                    nc.vector.tensor_copy(out=slot, in_=acc[:])
+                else:
+                    nc.scalar.copy(out=slot, in_=acc[:])
+                rows = out[2 * i * P : 2 * (i + 1) * P, c * CHUNK : (c + 1) * CHUNK]
+                nc.sync.dma_start(
+                    out=rows.rearrange("(u p) m -> p u m", u=2), in_=slot.rearrange("p (u m) -> p u m", u=2)
+                )
+
+        weave(0, 0)
+        weave(0, 1)
+        for c in range(chunks):
+            if c + 1 < chunks:
+                weave(c + 1, 0)
+            score(c)
+            if c + 1 < chunks:
+                weave(c + 1, 1)

@@ -15,6 +15,7 @@ U8 = mybir.dt.uint8
 FP8X4 = mybir.dt.float8_e4m3fn_x4
 FP4X4 = mybir.dt.float4_e2m1fn_x4
 MULT = mybir.AluOpType.mult
+ADD = mybir.AluOpType.add
 COPY = mybir.ActivationFunctionType.Copy
 TANH = mybir.ActivationFunctionType.Tanh
 
@@ -22,10 +23,15 @@ P = 128
 PACK = 4
 K_PASS = P * PACK
 QUADS = 4
+QUAD = P // QUADS
+SCALE_ROWS = 4
 BANK = 512
+BANKS = 8
 HALVES = T2 // BANK
-CHUNK = 256
+LIST_COLUMNS = S // 16
+LINE = 16
 ALIGN = 64
+CHUNKS = (256, 256, 256, 128, 128)
 
 
 def tile_list_flank_unrest_score_kernel(
@@ -47,21 +53,18 @@ def tile_list_flank_unrest_score_kernel(
         def bank(b, name):
             return psum.tile([P, BANK], F32, name=name, tag="bank%d" % b)
 
-        idx = lists.tile([P, S // 16], U16, name="idx")
-        idx2 = lists.tile([P, S // 16], U16, name="idx2")
-        idx3 = lists.tile([P, S // 16], U16, name="idx3")
-        idx4 = lists.tile([P, S // 16], U16, name="idx4")
+        idx = lists.tile([P, LIST_COLUMNS], U16, name="idx")
+        idx2 = lists.tile([P, LIST_COLUMNS], U16, name="idx2")
+        idx3 = lists.tile([P, LIST_COLUMNS], U16, name="idx3")
+        idx4 = lists.tile([P, LIST_COLUMNS], U16, name="idx4")
 
         tab_sc = tile([P, T], U8, "tab_sc")
         tab2_sc = tile([P, T], U8, "tab2_sc")
         w2_sc_raw = tile([P, passes2, H], U8, "w2_sc_raw")
         v2_sc_moved = tile([P, passes2 - 1, S], U8, "v2_sc_moved")
         w3_sc = tile([P, N], U8, "w3_sc")
-        nc.vector.memset(tab_sc[:].bitcast(I32), 0)
-        nc.vector.memset(tab2_sc[:].bitcast(I32), 0)
-        nc.vector.memset(w2_sc_raw[:].bitcast(I32), 0)
-        nc.vector.memset(w3_sc[:].bitcast(I32), 0)
-        nc.vector.memset(v2_sc_moved[:].bitcast(I32), 0)
+        for zeroed in (tab_sc, tab2_sc, w2_sc_raw, w3_sc, v2_sc_moved):
+            nc.vector.memset(zeroed[:].bitcast(I32), 0)
         page_a = [tile([P, T2], F32, "page_a%d" % i) for i in range(2)]
         page_b = [tile([P, T2], F32, "page_b%d" % i) for i in range(2)]
         for page in page_a + page_b:
@@ -72,16 +75,12 @@ def tile_list_flank_unrest_score_kernel(
         tab2 = [tile([P, T], I32, "tab2_%d" % a) for a in range(passes2)]
         w2_raw = tile([P, passes2, 2 * H], U8, "w2_raw")
         w3 = tile([P, N], I32, "w3")
-        w4_raw = tile([P, PACK, N], F32, "w4_raw")
-        e_pair = [tile([P, 2, T2], F32, "e_pair%d" % u) for u in range(2)]
-        e = [e_pair[t // 2][:, t % 2, :] for t in range(PACK)]
-        g1_first = tile([P, 2, S], F32, "g1_first")
-        g1_third = tile([P, 1, S], F32, "g1_third")
-        g2_all = tile([P, PACK, S], F32, "g2_all")
-        g1 = {0: g1_first[:, 0, :], 1: g1_first[:, 1, :], 2: g1_third[:, 0, :]}
-        g2 = [g2_all[:, t, :] for t in range(PACK)]
+        wg1_slice2 = tile([P, S], F32, "wg1_slice2")
+        wg1_rows = tile([P, S], F32, "wg1_rows", tag="h2_0")
+        wg2_rows = tile([P, S], F32, "wg2_rows", tag="h2_1")
         delay_sb = tile([P, PACK], F32, "delay_sb")
         gain_sb = tile([P, 2, PACK], F32, "gain_sb")
+        elev_slice = {}
 
         def load_w1(a):
             rows = w1[a * K_PASS : (a + 1) * K_PASS, :]
@@ -90,58 +89,76 @@ def tile_list_flank_unrest_score_kernel(
         def load_words(dst, words):
             nc.sync.dma_start(out=dst[:], in_=words.rearrange("p n i -> p (n i)").bitcast(I32))
 
-        def load_e(u):
-            nc.sync.dma_start(out=e_pair[u][:], in_=elev.rearrange("(p t) m -> p t m", t=PACK)[:, 2 * u : 2 * u + 2, :])
+        def load_elev_pair(u):
+            pair = tile([P, 2, T2], F32, "elev_pair%d" % u)
+            nc.sync.dma_start(out=pair[:], in_=elev.rearrange("(p t) m -> p t m", t=PACK)[:, 2 * u : 2 * u + 2, :])
+            for i in range(2):
+                elev_slice[2 * u + i] = pair[:, i, :]
 
-        def load_wg(dst, wg, t0, t1):
-            rows = wg.rearrange("(q t) j -> q (t j)", t=PACK)[:, t0 * S : t1 * S]
-            nc.sync.dma_start(
-                out=dst[:].rearrange("p t j -> p (t j)"),
-                in_=rows.unsqueeze(0).to_broadcast([QUADS, P // QUADS, (t1 - t0) * S]),
-            )
+        def load_wg1_slice(dst, t):
+            rows = wg1.rearrange("(q t) j -> q (t j)", t=PACK)[:, t * S : (t + 1) * S]
+            for q in (0, 2, 1, 3):
+                nc.sync.dma_start(out=dst[QUAD * q : QUAD * (q + 1)], in_=rows)
 
-        def load_packed_scales(engine, dst, scales):
+        def load_packed_planes(dst, scales):
             passes = scales.shape[0]
             for q in range(QUADS):
-                engine.dma_start(
-                    out=dst[32 * q : 32 * q + 4 * passes, :].bitcast(I32),
-                    in_=scales[:, 4 * q : 4 * q + 4, :].bitcast(I32),
-                )
-
-        def load_side_scales(engine, dst, scales):
-            for q in range(QUADS):
-                engine.dma_start(
-                    out=dst[32 * q : 32 * q + 4].bitcast(I32),
-                    in_=scales[:, 4 * q : 4 * q + 4, :].rearrange("a r c -> r a c").bitcast(I32),
-                )
-
-        nc.sync.dma_start(idx[:], offs)
-        load_w1(0)
-        load_packed_scales(nc.sync, tab_sc, tab_scales)
-        load_w1(1)
-        load_words(tab[0], tab_words[0])
-        nc.sync.dma_start(idx2[:], offs2)
-        load_packed_scales(nc.sync, tab2_sc, tab2_scales)
-        load_words(tab[1], tab_words[1])
-        nc.sync.dma_start(out=w2_raw[:].bitcast(I32), in_=w2_words.rearrange("a p c -> p a c").bitcast(I32))
-        nc.sync.dma_start(idx3[:], offs3)
-        load_wg(g1_first, wg1, 0, 2)
-        load_side_scales(nc.sync, w2_sc_raw, w2_scales)
-        load_e(0)
-        v_sc = tile([P, S], U8, "v_sc")
-        v2_sc = tile([P, S], U8, "v2_sc")
-        nc.vector.tensor_copy(v_sc[:], tab_sc[:].indirect(idx[:]))
-
-        def move_plane(a):
-            for q in range(QUADS):
                 nc.sync.dma_start(
-                    out=v2_sc_moved[32 * q : 32 * q + 4, a - 1, :].bitcast(I32),
-                    in_=v2_sc[32 * q + 4 * a : 32 * q + 4 * a + 4, :].bitcast(I32),
+                    out=dst[QUAD * q : QUAD * q + SCALE_ROWS * passes, :].bitcast(I32),
+                    in_=scales[:, SCALE_ROWS * q : SCALE_ROWS * (q + 1), :].bitcast(I32),
                 )
 
         ident = tile([P, P], F32, "ident")
         make_identity(nc, ident[:])
 
+        nc.sync.dma_start(idx[:], offs)
+        nc.sync.dma_start(idx2[:], offs2)
+        nc.sync.dma_start(out=wg1_rows[:], in_=wg1)
+        load_w1(0)
+        load_packed_planes(tab_sc, tab_scales)
+        nc.sync.dma_start(out=wg2_rows[:], in_=wg2)
+        load_w1(1)
+        load_words(tab[0], tab_words[0])
+        load_packed_planes(tab2_sc, tab2_scales)
+        load_words(tab[1], tab_words[1])
+        nc.sync.dma_start(out=w2_raw[:].bitcast(I32), in_=w2_words.rearrange("a p c -> p a c").bitcast(I32))
+        nc.sync.dma_start(idx3[:], offs3)
+        load_elev_pair(0)
+        for q in range(QUADS):
+            nc.sync.dma_start(
+                out=w2_sc_raw[QUAD * q : QUAD * q + SCALE_ROWS].bitcast(I32),
+                in_=w2_scales[:, SCALE_ROWS * q : SCALE_ROWS * (q + 1), :].rearrange("a r c -> r a c").bitcast(I32),
+            )
+
+        def turn(dst, src):
+            for j in range(BANK // P):
+                nc.tensor.transpose(dst[:, j * P : (j + 1) * P], src[:, j * P : (j + 1) * P], ident[:])
+
+        def repeat_wg(rows, count, b, name, tag):
+            turned = bank(b, name + "_turned")
+            turn(turned, rows)
+            repeated = tile([P, count, S // P, P], F32, name + "_repeated", tag=tag)
+            picked = turned[:].rearrange("p (c q t) -> p t c q", q=QUAD, t=PACK)[:, 0:count]
+            nc.scalar.copy(
+                out=repeated[:].rearrange("p t c (x q) -> p t c x q", x=QUADS),
+                in_=picked.unsqueeze(3).to_broadcast([P, count, S // P, QUADS, QUAD]),
+            )
+            return repeated
+
+        def deal_wg(repeated, t, b, name):
+            back = bank(b, name + "_back")
+            turn(back, repeated[:, t].rearrange("p c r -> p (c r)"))
+            dealt = tile([P, S], F32, name)
+            nc.scalar.copy(out=dealt[:], in_=back[:])
+            return dealt
+
+        wg1_repeated = repeat_wg(wg1_rows, 2, 4, "wg1", "w4_raw")
+        wg2_repeated = repeat_wg(wg2_rows, PACK, 5, "wg2", "elev_pair1")
+        wg1_slice = {t: deal_wg(wg1_repeated, t, 6 + t, "wg1_slice%d" % t) for t in range(2)}
+        wg1_slice[2] = wg1_slice2
+
+        v_sc = tile([P, S], U8, "v_sc")
+        v2_sc = tile([P, S], U8, "v2_sc")
         w1_codes = tile([P, passes1, H], U32, "w1_codes")
         w1_sc = tile([P, passes1, H], U8, "w1_sc")
         w1_bf = [tile([P, PACK * H], BF16, "w1_bf%d" % a) for a in range(passes1)]
@@ -151,37 +168,50 @@ def tile_list_flank_unrest_score_kernel(
         def gather_words(dst, table, offsets):
             nc.vector.tensor_copy(dst[:], table[:].bitcast(U32).indirect(offsets[:]))
 
-        for a in range(passes1):
-            nc.scalar.copy(
-                out=w1_bf[a][:].rearrange("p (t m j) -> p m j t", t=PACK, j=PACK),
-                in_=w1_raw[a][:].rearrange("p j (m t) -> p m j t", t=PACK),
-            )
-        nc.vector.quantize_mx(out=w1_codes[:, 0, :].bitcast(FP8X4), scales=w1_sc[:, 0, :], in_=w1_bf[0][:])
+        def quantize_w1(a):
+            nc.vector.quantize_mx(out=w1_codes[:, a, :].bitcast(FP8X4), scales=w1_sc[:, a, :], in_=w1_bf[a][:])
 
+        def move_plane(a):
+            for q in range(QUADS):
+                first = QUAD * q + SCALE_ROWS * a
+                nc.sync.dma_start(
+                    out=v2_sc_moved[QUAD * q : QUAD * q + SCALE_ROWS, a - 1, :].bitcast(I32),
+                    in_=v2_sc[first : first + SCALE_ROWS, :].bitcast(I32),
+                )
+
+        nc.vector.tensor_copy(v_sc[:], tab_sc[:].indirect(idx[:]))
+        for a, copy in enumerate((nc.vector.tensor_copy, nc.scalar.copy)):
+            copy(
+                out=w1_bf[a][:].rearrange("p (t m j) -> p m t j", t=PACK, j=PACK),
+                in_=w1_raw[a][:].rearrange("p j (m t) -> p m t j", t=PACK),
+            )
+        wg2_slice = [deal_wg(wg2_repeated, t, 4 + t, "wg2_slice%d" % t) for t in range(PACK)]
+        quantize_w1(0)
         gather_words(v[0], tab[0], idx)
-        nc.vector.quantize_mx(out=w1_codes[:, 1, :].bitcast(FP8X4), scales=w1_sc[:, 1, :], in_=w1_bf[1][:])
+        quantize_w1(1)
         nc.vector.tensor_copy(v2_sc[:], tab2_sc[:].indirect(idx2[:]))
         gather_words(v[1], tab[1], idx)
+
         w2_dealt = tile([P, passes2, 2 * H], U8, "w2_dealt")
         w2_sc = tile([P, passes2, H], U8, "w2_sc")
         nc.vector.tensor_copy(
-            out=w2_dealt[:].bitcast(U16).rearrange("p a (t m) -> p a m t", t=PACK),
-            in_=w2_raw[:].bitcast(U16).rearrange("p a (m t) -> p a m t", t=PACK),
+            out=w2_dealt[:].bitcast(U16).rearrange("p a (t g i) -> p a g t i", t=PACK, i=LINE // 2),
+            in_=w2_raw[:].bitcast(U16).rearrange("p a (g i t) -> p a g t i", t=PACK, i=LINE // 2),
         )
         nc.vector.tensor_copy(
-            out=w2_sc[:].rearrange("p a (t m) -> p a m t", t=PACK),
-            in_=w2_sc_raw[:].rearrange("p a (m t) -> p a m t", t=PACK),
+            out=w2_sc[:].rearrange("p a (t g i) -> p a g t i", t=PACK, i=LINE),
+            in_=w2_sc_raw[:].rearrange("p a (g i t) -> p a g t i", t=PACK, i=LINE),
         )
 
         load_words(tab2[0], tab2_words[0])
         load_words(tab2[1], tab2_words[1])
+        nc.sync.dma_start(out=delay_sb[:], in_=delay.rearrange("(p t) -> p t", t=PACK))
         move_plane(1)
         load_words(tab2[2], tab2_words[2])
         move_plane(2)
-        load_wg(g1_third, wg1, 2, 3)
-        load_wg(g2_all, wg2, 0, PACK)
-        nc.sync.dma_start(out=delay_sb[:], in_=delay.rearrange("(p t) -> p t", t=PACK))
+        load_wg1_slice(wg1_slice2, 2)
         nc.sync.dma_start(idx4[:], offs4)
+        load_elev_pair(1)
 
         h1_ps = [bank(t, "h1_ps%d" % t) for t in range(PACK)]
         for a in range(passes1):
@@ -190,7 +220,7 @@ def tile_list_flank_unrest_score_kernel(
                 nc.tensor.matmul_mx(
                     out=h1_ps[t][:],
                     lhsT=w1_codes[:, a, cols].bitcast(FP8X4), lhsT_scale=w1_sc[:, a, cols],
-                    rhs=v[a][:].bitcast(FP8X4), rhs_scale=v_sc[4 * a : P, :],
+                    rhs=v[a][:].bitcast(FP8X4), rhs_scale=v_sc[SCALE_ROWS * a : P, :],
                     start=(a == 0), stop=(a == passes1 - 1),
                 )
         h1 = [tile([P, S], F32, "h1_%d" % t) for t in range(PACK)]
@@ -199,11 +229,11 @@ def tile_list_flank_unrest_score_kernel(
             nc.scalar.activation(out=h1[t][:], in_=h1_ps[t][:], func=TANH)
 
         def scatter(page, offsets, h, wg):
-            nc.vector.tensor_tensor(page[:].indirect(offsets[:]), h[:], wg, MULT)
+            nc.vector.tensor_tensor(page[:].indirect(offsets[:]), h[:], wg[:], MULT)
 
-        def turned_sum(page, t, banks, name):
-            sums = [bank(b, "%s_%d" % (name, i)) for i, b in enumerate(banks)]
-            for term, src in enumerate((e[t], page)):
+        def turned_sum(page, t, first_bank, name):
+            sums = [bank(first_bank + half, "%s_%d" % (name, half)) for half in range(HALVES)]
+            for term, src in enumerate((elev_slice[t], page)):
                 for half in range(HALVES):
                     for j in range(BANK // P):
                         m0 = half * BANK + j * P
@@ -214,47 +244,45 @@ def tile_list_flank_unrest_score_kernel(
                         )
             return sums
 
-        held_tags = ["w1_raw0", "w1_raw1", "w1_bf0", "w1_bf1"]
-
-        def hold(sums, t):
-            held = tile([P, HALVES, BANK], F32, "held%d" % t, tag=held_tags[t])
+        def hold(sums, t, tag):
+            held = tile([P, HALVES, BANK], F32, "held%d" % t, tag=tag)
             for half in range(HALVES):
                 nc.scalar.copy(out=held[:, half, :], in_=sums[half][:])
             return held
 
-        zs_planes = [tile([P, PACK, BANK], BF16, "zs_planes%d" % i) for i in range(HALVES)]
-        zt_planes = [tile([P, PACK, BANK], BF16, "zt_planes%d" % i) for i in range(HALVES)]
+        zs_slices = [tile([P, PACK, BANK], BF16, "zs_slices%d" % half) for half in range(HALVES)]
+        zt_slices = [tile([P, PACK, BANK], BF16, "zt_slices%d" % half) for half in range(HALVES)]
 
-        def product(sums, held, t, banks):
+        def gains(z, t, half):
+            tag = "w4_raw" if (t, half) == (0, 0) else "tanh_z%d" % half
+            tanh_z = tile([P, BANK], F32, "tanh_z%d" % half, tag=tag)
+            nc.scalar.activation(out=zs_slices[half][:, t, :], in_=z[:], func=COPY, scale=gain_sb[:, 0, t : t + 1])
+            nc.scalar.activation(out=tanh_z[:], in_=z[:], func=TANH)
+            nc.scalar.activation(out=zt_slices[half][:, t, :], in_=tanh_z[:], func=COPY, scale=gain_sb[:, 1, t : t + 1])
+
+        def product(sums, held, t, first_bank):
             for half in range(HALVES):
                 z_turned = tile([P, BANK], F32, "z_turned%d" % half)
                 nc.vector.tensor_tensor(z_turned[:], sums[half][:], held[:, half, :], MULT)
-                z = bank(banks[half], "z%d_%d" % (t, half))
-                for j in range(BANK // P):
-                    nc.tensor.transpose(z[:, j * P : (j + 1) * P], z_turned[:, j * P : (j + 1) * P], ident[:])
-                tag = "w4_raw" if (t, half) == (0, 0) else "tanh_z%d" % half
-                tanh_z = tile([P, BANK], F32, "tanh_z%d" % half, tag=tag)
-                nc.scalar.activation(out=zs_planes[half][:, t, :], in_=z[:], func=COPY, scale=gain_sb[:, 0, t : t + 1])
-                nc.scalar.activation(out=tanh_z[:], in_=z[:], func=TANH)
-                nc.scalar.activation(
-                    out=zt_planes[half][:, t, :], in_=tanh_z[:], func=COPY, scale=gain_sb[:, 1, t : t + 1]
-                )
+                z = bank(first_bank + half, "z%d_%d" % (t, half))
+                turn(z, z_turned)
+                gains(z, t, half)
 
         held = {}
         for t in range(2):
-            scatter(page_a[t], idx3, h1[t], g1[t])
-            held[t] = hold(turned_sum(page_a[t], t, (4 + 2 * t, 5 + 2 * t), "a%d" % t), t)
+            scatter(page_a[t], idx3, h1[t], wg1_slice[t])
+            held[t] = hold(turned_sum(page_a[t], t, 4 + 2 * t, "a%d" % t), t, "w1_raw%d" % t)
 
         for a in range(passes2):
             gather_words(v2[a], tab2[a], idx2)
-        load_e(1)
+        w4_raw = tile([P, PACK, N], F32, "w4_raw")
         nc.sync.dma_start(out=w4_raw[:], in_=w4.rearrange("(p j) c -> p j c", j=PACK))
         nc.sync.dma_start(out=gain_sb[:], in_=gain.rearrange("(s p t) -> p s t", s=2, t=PACK))
         load_words(w3, w3_words[0])
         for q in range(QUADS):
             nc.sync.dma_start(
-                out=w3_sc[32 * q : 32 * q + 4, :].bitcast(I32),
-                in_=w3_scales[0, 4 * q : 4 * q + 4, :].bitcast(I32),
+                out=w3_sc[QUAD * q : QUAD * q + SCALE_ROWS, :].bitcast(I32),
+                in_=w3_scales[0, SCALE_ROWS * q : SCALE_ROWS * (q + 1), :].bitcast(I32),
             )
         h2_ps = [bank(t, "h2_ps%d" % t) for t in range(PACK)]
         for t in range(PACK):
@@ -269,91 +297,109 @@ def tile_list_flank_unrest_score_kernel(
                 )
             nc.scalar.activation(out=h2[t][:], in_=h2_ps[t][:], func=COPY, scale=delay_sb[:, t : t + 1])
 
-        scatter(page_a[0], idx3, h1[2], g1[2])
-        held[2] = hold(turned_sum(page_a[0], 2, (4, 5), "a2"), 2)
+        scatter(page_a[0], idx3, h1[2], wg1_slice[2])
+        held[2] = hold(turned_sum(page_a[0], 2, 4, "a2"), 2, "w1_bf0")
 
-        scatter(page_b[0], idx4, h2[0], g2[0])
-        sums_b0 = turned_sum(page_b[0], 0, (6, 7), "b0")
+        scatter(page_b[0], idx4, h2[0], wg2_slice[0])
+        sums_b0 = turned_sum(page_b[0], 0, 6, "b0")
         w4_bf = tile([P, PACK * N], BF16, "w4_bf", tag="h2_0")
         nc.scalar.copy(
-            out=w4_bf[:].rearrange("p (c i j) -> p c j i", i=4, j=PACK),
-            in_=w4_raw[:].rearrange("p j (c i) -> p c j i", i=4),
+            out=w4_bf[:].rearrange("p (c j) -> p c j", j=PACK),
+            in_=w4_raw[:].rearrange("p j c -> p c j"),
         )
-        scatter(page_b[1], idx4, h2[1], g2[1])
-        sums_b1 = turned_sum(page_b[1], 1, (0, 1), "b1")
-        product(sums_b0, held[0], 0, (2, 3))
-        scatter(page_b[0], idx4, h2[2], g2[2])
-        sums_b2 = turned_sum(page_b[0], 2, (4, 5), "b2")
-        product(sums_b1, held[1], 1, (6, 7))
-        g1_last = tile([P, 1, S], F32, "g1_last", tag=held_tags[1])
-        load_wg(g1_last, wg1, 3, 4)
-        g1[3] = g1_last[:, 0, :]
-        w4_codes = tile([P, N], U32, "w4_codes", tag=held_tags[0])
+        scatter(page_b[1], idx4, h2[1], wg2_slice[1])
+        sums_b1 = turned_sum(page_b[1], 1, 0, "b1")
+        product(sums_b0, held[0], 0, 2)
+        scatter(page_b[0], idx4, h2[2], wg2_slice[2])
+        wg1_slice[3] = tile([P, S], F32, "wg1_slice3", tag="h2_2")
+        load_wg1_slice(wg1_slice[3], 3)
+        sums_b2 = turned_sum(page_b[0], 2, 4, "b2")
+        product(sums_b1, held[1], 1, 6)
+        w4_codes = tile([P, N], U32, "w4_codes", tag="w1_raw0")
         w4_sc = tile([P, N], U8, "w4_sc")
-        for c0, c1 in ((0, 512), (512, N)):
+        for c0, c1 in ((0, K_PASS), (K_PASS, N)):
             nc.vector.quantize_mx(
                 out=w4_codes[:, c0:c1].bitcast(FP8X4), scales=w4_sc[:, c0:c1], in_=w4_bf[:, PACK * c0 : PACK * c1]
             )
-        scatter(page_b[1], idx4, h2[3], g2[3])
-        held[3] = hold(turned_sum(page_b[1], 3, (0, 1), "b3"), 3)
-        product(sums_b2, held[2], 2, (2, 3))
-        scatter(page_a[1], idx3, h1[3], g1[3])
-        sums_a3 = turned_sum(page_a[1], 3, (4, 5), "a3")
-        product(sums_a3, held[3], 3, (6, 7))
+        scatter(page_b[1], idx4, h2[3], wg2_slice[3])
+        product(sums_b2, held[2], 2, 2)
 
-        chunks = T2 // CHUNK
-        pairs = N // (2 * P)
+        sum_b3 = tile([P, T2], F32, "sum_b3", tag="w1_bf1")
+        nc.vector.tensor_tensor(sum_b3[:], page_b[1][:], elev_slice[3], ADD)
+        scatter(page_a[1], idx3, h1[3], wg1_slice[3])
+        sum_a3 = [tile([P, BANK], F32, "sum_a3_%d" % half, tag="h1_%d" % half) for half in range(HALVES)]
+        for half in range(HALVES):
+            cols = slice(half * BANK, (half + 1) * BANK)
+            nc.vector.tensor_tensor(sum_a3[half][:], page_a[1][:, cols], elev_slice[3][:, cols], ADD)
+        for half in range(HALVES):
+            cols = slice(half * BANK, (half + 1) * BANK)
+            z3 = tile([P, BANK], F32, "z3_%d" % half, tag="z_turned%d" % half)
+            nc.vector.tensor_tensor(z3[:], sum_a3[half][:], sum_b3[:, cols], MULT)
+            gains(z3, 3, half)
+
+        starts = [sum(CHUNKS[:c]) for c in range(len(CHUNKS))]
+        per_bank = [2 if width == max(CHUNKS) else 3 for width in CHUNKS]
         staged = [
-            tile([P, width, BANK], F32, "staged_" + tag, tag=tag)
-            for tag, width in (("e_pair0", 4), ("w4_raw", 6), ("g2_all", 2))
+            tile([P, count, BANK], F32, "staged_" + tag, tag=tag)
+            for tag, count in (
+                ("elev_pair0", 4), ("w4_raw", 6), ("wg2_slice0", 1), ("wg2_slice1", 1), ("wg2_slice2", 1),
+            )
         ]
-        slots = [st[:, i, :] for st in staged for i in range(st.shape[1])]
+        staging_rows = [st[:, i, :] for st in staged for i in range(st.shape[1])]
+        first_acc = [sum(N // P // count for count in per_bank[:c]) for c in range(len(CHUNKS))]
         woven = {}
+        accs = {}
 
         def weave(c, s):
-            if s == 0:
-                woven[c] = tile([P, 2, PACK * CHUNK], BF16, "woven", bufs=2)
-            planes = (zs_planes, zt_planes)[s][c * CHUNK // BANK]
-            m0 = c * CHUNK % BANK
+            woven[c, s] = tile([P, PACK * CHUNKS[c]], BF16, "woven", bufs=4)
+            slices = (zs_slices, zt_slices)[s][starts[c] // BANK]
+            m0 = starts[c] % BANK
             nc.vector.tensor_copy(
-                out=woven[c][:, s, :].rearrange("p (c i t) -> p c t i", i=4, t=PACK),
-                in_=planes[:, :, m0 : m0 + CHUNK].rearrange("p t (c i) -> p c t i", i=4),
+                out=woven[c, s][:].rearrange("p (m t) -> p m t", t=PACK),
+                in_=slices[:, :, m0 : m0 + CHUNKS[c]].rearrange("p t m -> p m t"),
             )
 
-        def score(c):
-            codes = tile([P, 2, CHUNK], U32, "z_codes", bufs=2)
-            scales = tile([P, 2, CHUNK], U8, "z_sc", bufs=2)
-            nc.vector.quantize_mx(
-                out=codes[:].rearrange("p s m -> p (s m)").bitcast(FP8X4),
-                scales=scales[:].rearrange("p s m -> p (s m)"),
-                in_=woven[c][:].rearrange("p s x -> p (s x)"),
-            )
-            for i in range(pairs):
-                acc = bank((pairs * c + i) % 8, "acc%d_%d" % (c, i))
-                for u in range(2):
-                    cols = slice((2 * i + u) * P, (2 * i + u + 1) * P)
-                    for s, (w_codes, w_sc) in enumerate(((w3, w3_sc), (w4_codes, w4_sc))):
-                        nc.tensor.matmul_mx(
-                            out=acc[:, u * CHUNK : (u + 1) * CHUNK],
-                            lhsT=w_codes[:, cols].bitcast(FP8X4), lhsT_scale=w_sc[:, cols],
-                            rhs=codes[:, s, :].bitcast(FP8X4), rhs_scale=scales[:, s, :],
-                            start=(s == 0), stop=(s == 1),
-                        )
-                slot = slots[pairs * c + i]
-                if c == chunks - 1 and i != 1:
-                    nc.vector.tensor_copy(out=slot, in_=acc[:])
+        def multiply(c, s):
+            width = CHUNKS[c]
+            codes = tile([P, width], U32, "z_codes", bufs=2 * len(CHUNKS))
+            scales = tile([P, width], U8, "z_sc", bufs=2 * len(CHUNKS))
+            nc.vector.quantize_mx(out=codes[:].bitcast(FP8X4), scales=scales[:], in_=woven[c, s][:])
+            w_codes, w_sc = ((w3, w3_sc), (w4_codes, w4_sc))[s]
+            for i in range(N // P // per_bank[c]):
+                if s == 0:
+                    accs[c, i] = bank((first_acc[c] + i) % BANKS, "acc%d_%d" % (c, i))
+                for u in range(per_bank[c]):
+                    n0 = (per_bank[c] * i + u) * P
+                    nc.tensor.matmul_mx(
+                        out=accs[c, i][:, u * width : (u + 1) * width],
+                        lhsT=w_codes[:, n0 : n0 + P].bitcast(FP8X4), lhsT_scale=w_sc[:, n0 : n0 + P],
+                        rhs=codes[:].bitcast(FP8X4), rhs_scale=scales[:],
+                        start=(s == 0 and u == 0), stop=(s == 1 and u == per_bank[c] - 1),
+                    )
+
+        def store(c):
+            width = CHUNKS[c]
+            used = per_bank[c] * width
+            for i in range(N // P // per_bank[c]):
+                row = staging_rows[first_acc[c] + i][:, 0:used]
+                if width < max(CHUNKS) and i == 1:
+                    nc.vector.tensor_copy(out=row, in_=accs[c, i][:, 0:used])
                 else:
-                    nc.scalar.copy(out=slot, in_=acc[:])
-                rows = out[2 * i * P : 2 * (i + 1) * P, c * CHUNK : (c + 1) * CHUNK]
+                    nc.scalar.copy(out=row, in_=accs[c, i][:, 0:used])
+                n0 = per_bank[c] * i * P
+                block = out[n0 : n0 + per_bank[c] * P, starts[c] : starts[c] + width]
                 nc.sync.dma_start(
-                    out=rows.rearrange("(u p) m -> p u m", u=2), in_=slot.rearrange("p (u m) -> p u m", u=2)
+                    out=block.rearrange("(u p) m -> p u m", u=per_bank[c]),
+                    in_=row.rearrange("p (u m) -> p u m", u=per_bank[c]),
                 )
 
         weave(0, 0)
-        weave(0, 1)
-        for c in range(chunks):
-            if c + 1 < chunks:
+        multiply(0, 0)
+        for c in range(len(CHUNKS)):
+            weave(c, 1)
+            if c + 1 < len(CHUNKS):
                 weave(c + 1, 0)
-            score(c)
-            if c + 1 < chunks:
-                weave(c + 1, 1)
+            multiply(c, 1)
+            store(c)
+            if c + 1 < len(CHUNKS):
+                multiply(c + 1, 0)

from contextlib import ExitStack

import concourse.mybir as mybir
from concourse.masks import make_identity

K1, K2, H, N, T, S, T2 = 1024, 1536, 512, 768, 2048, 512, 1024
FLOPS = 2 * (K1 * H * S + K2 * H * S + 2 * H * N * T2)

F32 = mybir.dt.float32
BF16 = mybir.dt.bfloat16
I32 = mybir.dt.int32
U32 = mybir.dt.uint32
U16 = mybir.dt.uint16
U8 = mybir.dt.uint8
FP8X4 = mybir.dt.float8_e4m3fn_x4
FP4X4 = mybir.dt.float4_e2m1fn_x4
MULT = mybir.AluOpType.mult
ADD = mybir.AluOpType.add
COPY = mybir.ActivationFunctionType.Copy
TANH = mybir.ActivationFunctionType.Tanh

P = 128
PACK = 4
K_PASS = P * PACK
QUADS = 4
QUAD = P // QUADS
SCALE_ROWS = 4
BANK = 512
BANKS = 8
HALVES = T2 // BANK
LIST_COLUMNS = S // 16
LINE = 16
ALIGN = 64
CHUNKS = (256, 256, 256, 128, 128)


def tile_list_flank_unrest_score_kernel(
    tc, tab_words, tab_scales, tab2_words, tab2_scales, offs, offs2, offs3, offs4,
    w1, w2_words, w2_scales, w3_words, w3_scales, w4, delay, gain, elev, wg1, wg2, out,
):
    nc = tc.nc
    passes1 = K1 // K_PASS
    passes2 = K2 // K_PASS

    with ExitStack() as ctx:
        lists = ctx.enter_context(tc.tile_pool(name="lists", bufs=1))
        sb = ctx.enter_context(tc.tile_pool(name="sb", bufs=1))
        psum = ctx.enter_context(tc.psum_pool(name="psum", bufs=1))

        def tile(shape, dtype, name, tag=None, bufs=1):
            return sb.tile(shape, dtype, name=name, tag=tag or name, bufs=bufs, align_bytes=ALIGN)

        def bank(b, name):
            return psum.tile([P, BANK], F32, name=name, tag="bank%d" % b)

        idx = lists.tile([P, LIST_COLUMNS], U16, name="idx")
        idx2 = lists.tile([P, LIST_COLUMNS], U16, name="idx2")
        idx3 = lists.tile([P, LIST_COLUMNS], U16, name="idx3")
        idx4 = lists.tile([P, LIST_COLUMNS], U16, name="idx4")

        tab_sc = tile([P, T], U8, "tab_sc")
        tab2_sc = tile([P, T], U8, "tab2_sc")
        w2_sc_raw = tile([P, passes2, H], U8, "w2_sc_raw")
        v2_sc_moved = tile([P, passes2 - 1, S], U8, "v2_sc_moved")
        w3_sc = tile([P, N], U8, "w3_sc")
        for zeroed in (tab_sc, tab2_sc, w2_sc_raw, w3_sc, v2_sc_moved):
            nc.vector.memset(zeroed[:].bitcast(I32), 0)
        page_a = [tile([P, T2], F32, "page_a%d" % i) for i in range(2)]
        page_b = [tile([P, T2], F32, "page_b%d" % i) for i in range(2)]
        for page in page_a + page_b:
            nc.vector.memset(page[:], 0.0)

        w1_raw = [tile([P, PACK, H], F32, "w1_raw%d" % a) for a in range(passes1)]
        tab = [tile([P, T], I32, "tab_%d" % a) for a in range(passes1)]
        tab2 = [tile([P, T], I32, "tab2_%d" % a) for a in range(passes2)]
        w2_raw = tile([P, passes2, 2 * H], U8, "w2_raw")
        w3 = tile([P, N], I32, "w3")
        wg1_slice2 = tile([P, S], F32, "wg1_slice2")
        wg1_rows = tile([P, S], F32, "wg1_rows", tag="h2_0")
        wg2_rows = tile([P, S], F32, "wg2_rows", tag="h2_1")
        delay_sb = tile([P, PACK], F32, "delay_sb")
        gain_sb = tile([P, 2, PACK], F32, "gain_sb")
        elev_slice = {}

        def load_w1(a):
            rows = w1[a * K_PASS : (a + 1) * K_PASS, :]
            nc.sync.dma_start(out=w1_raw[a][:], in_=rows.rearrange("(p j) c -> p j c", j=PACK))

        def load_words(dst, words):
            nc.sync.dma_start(out=dst[:], in_=words.rearrange("p n i -> p (n i)").bitcast(I32))

        def load_elev_pair(u):
            pair = tile([P, 2, T2], F32, "elev_pair%d" % u)
            nc.sync.dma_start(out=pair[:], in_=elev.rearrange("(p t) m -> p t m", t=PACK)[:, 2 * u : 2 * u + 2, :])
            for i in range(2):
                elev_slice[2 * u + i] = pair[:, i, :]

        def load_wg1_slice(dst, t):
            rows = wg1.rearrange("(q t) j -> q (t j)", t=PACK)[:, t * S : (t + 1) * S]
            for q in (0, 2, 1, 3):
                nc.sync.dma_start(out=dst[QUAD * q : QUAD * (q + 1)], in_=rows)

        def load_packed_planes(dst, scales):
            passes = scales.shape[0]
            for q in range(QUADS):
                nc.sync.dma_start(
                    out=dst[QUAD * q : QUAD * q + SCALE_ROWS * passes, :].bitcast(I32),
                    in_=scales[:, SCALE_ROWS * q : SCALE_ROWS * (q + 1), :].bitcast(I32),
                )

        ident = tile([P, P], F32, "ident")
        make_identity(nc, ident[:])

        nc.sync.dma_start(idx[:], offs)
        nc.sync.dma_start(idx2[:], offs2)
        nc.sync.dma_start(out=wg1_rows[:], in_=wg1)
        load_w1(0)
        load_packed_planes(tab_sc, tab_scales)
        nc.sync.dma_start(out=wg2_rows[:], in_=wg2)
        load_w1(1)
        load_words(tab[0], tab_words[0])
        load_packed_planes(tab2_sc, tab2_scales)
        load_words(tab[1], tab_words[1])
        nc.sync.dma_start(out=w2_raw[:].bitcast(I32), in_=w2_words.rearrange("a p c -> p a c").bitcast(I32))
        nc.sync.dma_start(idx3[:], offs3)
        load_elev_pair(0)
        for q in range(QUADS):
            nc.sync.dma_start(
                out=w2_sc_raw[QUAD * q : QUAD * q + SCALE_ROWS].bitcast(I32),
                in_=w2_scales[:, SCALE_ROWS * q : SCALE_ROWS * (q + 1), :].rearrange("a r c -> r a c").bitcast(I32),
            )

        def turn(dst, src):
            for j in range(BANK // P):
                nc.tensor.transpose(dst[:, j * P : (j + 1) * P], src[:, j * P : (j + 1) * P], ident[:])

        def repeat_wg(rows, count, b, name, tag):
            turned = bank(b, name + "_turned")
            turn(turned, rows)
            repeated = tile([P, count, S // P, P], F32, name + "_repeated", tag=tag)
            picked = turned[:].rearrange("p (c q t) -> p t c q", q=QUAD, t=PACK)[:, 0:count]
            nc.scalar.copy(
                out=repeated[:].rearrange("p t c (x q) -> p t c x q", x=QUADS),
                in_=picked.unsqueeze(3).to_broadcast([P, count, S // P, QUADS, QUAD]),
            )
            return repeated

        def deal_wg(repeated, t, b, name):
            back = bank(b, name + "_back")
            turn(back, repeated[:, t].rearrange("p c r -> p (c r)"))
            dealt = tile([P, S], F32, name)
            nc.scalar.copy(out=dealt[:], in_=back[:])
            return dealt

        wg1_repeated = repeat_wg(wg1_rows, 2, 4, "wg1", "w4_raw")
        wg2_repeated = repeat_wg(wg2_rows, PACK, 5, "wg2", "elev_pair1")
        wg1_slice = {t: deal_wg(wg1_repeated, t, 6 + t, "wg1_slice%d" % t) for t in range(2)}
        wg1_slice[2] = wg1_slice2

        v_sc = tile([P, S], U8, "v_sc")
        v2_sc = tile([P, S], U8, "v2_sc")
        w1_codes = tile([P, passes1, H], U32, "w1_codes")
        w1_sc = tile([P, passes1, H], U8, "w1_sc")
        w1_bf = [tile([P, PACK * H], BF16, "w1_bf%d" % a) for a in range(passes1)]
        v = [tile([P, S], U32, "v_%d" % a) for a in range(passes1)]
        v2 = [tile([P, S], U32, "v2_%d" % a) for a in range(passes2)]

        def gather_words(dst, table, offsets):
            nc.vector.tensor_copy(dst[:], table[:].bitcast(U32).indirect(offsets[:]))

        def quantize_w1(a):
            nc.vector.quantize_mx(out=w1_codes[:, a, :].bitcast(FP8X4), scales=w1_sc[:, a, :], in_=w1_bf[a][:])

        def move_plane(a):
            for q in range(QUADS):
                first = QUAD * q + SCALE_ROWS * a
                nc.sync.dma_start(
                    out=v2_sc_moved[QUAD * q : QUAD * q + SCALE_ROWS, a - 1, :].bitcast(I32),
                    in_=v2_sc[first : first + SCALE_ROWS, :].bitcast(I32),
                )

        nc.vector.tensor_copy(v_sc[:], tab_sc[:].indirect(idx[:]))
        for a, copy in enumerate((nc.vector.tensor_copy, nc.scalar.copy)):
            copy(
                out=w1_bf[a][:].rearrange("p (t m j) -> p m t j", t=PACK, j=PACK),
                in_=w1_raw[a][:].rearrange("p j (m t) -> p m t j", t=PACK),
            )
        wg2_slice = [deal_wg(wg2_repeated, t, 4 + t, "wg2_slice%d" % t) for t in range(PACK)]
        quantize_w1(0)
        gather_words(v[0], tab[0], idx)
        quantize_w1(1)
        nc.vector.tensor_copy(v2_sc[:], tab2_sc[:].indirect(idx2[:]))
        gather_words(v[1], tab[1], idx)

        w2_dealt = tile([P, passes2, 2 * H], U8, "w2_dealt")
        w2_sc = tile([P, passes2, H], U8, "w2_sc")
        nc.vector.tensor_copy(
            out=w2_dealt[:].bitcast(U16).rearrange("p a (t g i) -> p a g t i", t=PACK, i=LINE // 2),
            in_=w2_raw[:].bitcast(U16).rearrange("p a (g i t) -> p a g t i", t=PACK, i=LINE // 2),
        )
        nc.vector.tensor_copy(
            out=w2_sc[:].rearrange("p a (t g i) -> p a g t i", t=PACK, i=LINE),
            in_=w2_sc_raw[:].rearrange("p a (g i t) -> p a g t i", t=PACK, i=LINE),
        )

        load_words(tab2[0], tab2_words[0])
        load_words(tab2[1], tab2_words[1])
        nc.sync.dma_start(out=delay_sb[:], in_=delay.rearrange("(p t) -> p t", t=PACK))
        move_plane(1)
        load_words(tab2[2], tab2_words[2])
        move_plane(2)
        load_wg1_slice(wg1_slice2, 2)
        nc.sync.dma_start(idx4[:], offs4)
        load_elev_pair(1)

        h1_ps = [bank(t, "h1_ps%d" % t) for t in range(PACK)]
        for a in range(passes1):
            for t in range(PACK):
                cols = slice(t * P, (t + 1) * P)
                nc.tensor.matmul_mx(
                    out=h1_ps[t][:],
                    lhsT=w1_codes[:, a, cols].bitcast(FP8X4), lhsT_scale=w1_sc[:, a, cols],
                    rhs=v[a][:].bitcast(FP8X4), rhs_scale=v_sc[SCALE_ROWS * a : P, :],
                    start=(a == 0), stop=(a == passes1 - 1),
                )
        h1 = [tile([P, S], F32, "h1_%d" % t) for t in range(PACK)]
        h2 = [tile([P, S], F32, "h2_%d" % t) for t in range(PACK)]
        for t in range(PACK):
            nc.scalar.activation(out=h1[t][:], in_=h1_ps[t][:], func=TANH)

        def scatter(page, offsets, h, wg):
            nc.vector.tensor_tensor(page[:].indirect(offsets[:]), h[:], wg[:], MULT)

        def turned_sum(page, t, first_bank, name):
            sums = [bank(first_bank + half, "%s_%d" % (name, half)) for half in range(HALVES)]
            for term, src in enumerate((elev_slice[t], page)):
                for half in range(HALVES):
                    for j in range(BANK // P):
                        m0 = half * BANK + j * P
                        nc.tensor.matmul(
                            out=sums[half][:, j * P : (j + 1) * P], lhsT=src[:, m0 : m0 + P], rhs=ident[:],
                            is_transpose=True,
                            start=(term == 0 and j == 0), stop=(term == 1 and j == BANK // P - 1),
                        )
            return sums

        def hold(sums, t, tag):
            held = tile([P, HALVES, BANK], F32, "held%d" % t, tag=tag)
            for half in range(HALVES):
                nc.scalar.copy(out=held[:, half, :], in_=sums[half][:])
            return held

        zs_slices = [tile([P, PACK, BANK], BF16, "zs_slices%d" % half) for half in range(HALVES)]
        zt_slices = [tile([P, PACK, BANK], BF16, "zt_slices%d" % half) for half in range(HALVES)]

        def gains(z, t, half):
            tag = "w4_raw" if (t, half) == (0, 0) else "tanh_z%d" % half
            tanh_z = tile([P, BANK], F32, "tanh_z%d" % half, tag=tag)
            nc.scalar.activation(out=zs_slices[half][:, t, :], in_=z[:], func=COPY, scale=gain_sb[:, 0, t : t + 1])
            nc.scalar.activation(out=tanh_z[:], in_=z[:], func=TANH)
            nc.scalar.activation(out=zt_slices[half][:, t, :], in_=tanh_z[:], func=COPY, scale=gain_sb[:, 1, t : t + 1])

        def product(sums, held, t, first_bank):
            for half in range(HALVES):
                z_turned = tile([P, BANK], F32, "z_turned%d" % half)
                nc.vector.tensor_tensor(z_turned[:], sums[half][:], held[:, half, :], MULT)
                z = bank(first_bank + half, "z%d_%d" % (t, half))
                turn(z, z_turned)
                gains(z, t, half)

        held = {}
        for t in range(2):
            scatter(page_a[t], idx3, h1[t], wg1_slice[t])
            held[t] = hold(turned_sum(page_a[t], t, 4 + 2 * t, "a%d" % t), t, "w1_raw%d" % t)

        for a in range(passes2):
            gather_words(v2[a], tab2[a], idx2)
        w4_raw = tile([P, PACK, N], F32, "w4_raw")
        nc.sync.dma_start(out=w4_raw[:], in_=w4.rearrange("(p j) c -> p j c", j=PACK))
        nc.sync.dma_start(out=gain_sb[:], in_=gain.rearrange("(s p t) -> p s t", s=2, t=PACK))
        load_words(w3, w3_words[0])
        for q in range(QUADS):
            nc.sync.dma_start(
                out=w3_sc[QUAD * q : QUAD * q + SCALE_ROWS, :].bitcast(I32),
                in_=w3_scales[0, SCALE_ROWS * q : SCALE_ROWS * (q + 1), :].bitcast(I32),
            )
        h2_ps = [bank(t, "h2_ps%d" % t) for t in range(PACK)]
        for t in range(PACK):
            cols = slice(t * P, (t + 1) * P)
            for a in range(passes2):
                nc.tensor.matmul_mx(
                    out=h2_ps[t][:],
                    lhsT=w2_dealt[:, a, 2 * t * P : 2 * (t + 1) * P].bitcast(FP4X4), lhsT_scale=w2_sc[:, a, cols],
                    rhs=v2[a][:].bitcast(FP8X4),
                    rhs_scale=v2_sc[:] if a == 0 else v2_sc_moved[:, a - 1, :],
                    start=(a == 0), stop=(a == passes2 - 1),
                )
            nc.scalar.activation(out=h2[t][:], in_=h2_ps[t][:], func=COPY, scale=delay_sb[:, t : t + 1])

        scatter(page_a[0], idx3, h1[2], wg1_slice[2])
        held[2] = hold(turned_sum(page_a[0], 2, 4, "a2"), 2, "w1_bf0")

        scatter(page_b[0], idx4, h2[0], wg2_slice[0])
        sums_b0 = turned_sum(page_b[0], 0, 6, "b0")
        w4_bf = tile([P, PACK * N], BF16, "w4_bf", tag="h2_0")
        nc.scalar.copy(
            out=w4_bf[:].rearrange("p (c j) -> p c j", j=PACK),
            in_=w4_raw[:].rearrange("p j c -> p c j"),
        )
        scatter(page_b[1], idx4, h2[1], wg2_slice[1])
        sums_b1 = turned_sum(page_b[1], 1, 0, "b1")
        product(sums_b0, held[0], 0, 2)
        scatter(page_b[0], idx4, h2[2], wg2_slice[2])
        wg1_slice[3] = tile([P, S], F32, "wg1_slice3", tag="h2_2")
        load_wg1_slice(wg1_slice[3], 3)
        sums_b2 = turned_sum(page_b[0], 2, 4, "b2")
        product(sums_b1, held[1], 1, 6)
        w4_codes = tile([P, N], U32, "w4_codes", tag="w1_raw0")
        w4_sc = tile([P, N], U8, "w4_sc")
        for c0, c1 in ((0, K_PASS), (K_PASS, N)):
            nc.vector.quantize_mx(
                out=w4_codes[:, c0:c1].bitcast(FP8X4), scales=w4_sc[:, c0:c1], in_=w4_bf[:, PACK * c0 : PACK * c1]
            )
        scatter(page_b[1], idx4, h2[3], wg2_slice[3])
        product(sums_b2, held[2], 2, 2)

        sum_b3 = tile([P, T2], F32, "sum_b3", tag="w1_bf1")
        nc.vector.tensor_tensor(sum_b3[:], page_b[1][:], elev_slice[3], ADD)
        scatter(page_a[1], idx3, h1[3], wg1_slice[3])
        sum_a3 = [tile([P, BANK], F32, "sum_a3_%d" % half, tag="h1_%d" % half) for half in range(HALVES)]
        for half in range(HALVES):
            cols = slice(half * BANK, (half + 1) * BANK)
            nc.vector.tensor_tensor(sum_a3[half][:], page_a[1][:, cols], elev_slice[3][:, cols], ADD)
        for half in range(HALVES):
            cols = slice(half * BANK, (half + 1) * BANK)
            z3 = tile([P, BANK], F32, "z3_%d" % half, tag="z_turned%d" % half)
            nc.vector.tensor_tensor(z3[:], sum_a3[half][:], sum_b3[:, cols], MULT)
            gains(z3, 3, half)

        starts = [sum(CHUNKS[:c]) for c in range(len(CHUNKS))]
        per_bank = [2 if width == max(CHUNKS) else 3 for width in CHUNKS]
        staged = [
            tile([P, count, BANK], F32, "staged_" + tag, tag=tag)
            for tag, count in (
                ("elev_pair0", 4), ("w4_raw", 6), ("wg2_slice0", 1), ("wg2_slice1", 1), ("wg2_slice2", 1),
            )
        ]
        staging_rows = [st[:, i, :] for st in staged for i in range(st.shape[1])]
        first_acc = [sum(N // P // count for count in per_bank[:c]) for c in range(len(CHUNKS))]
        woven = {}
        accs = {}

        def weave(c, s):
            woven[c, s] = tile([P, PACK * CHUNKS[c]], BF16, "woven", bufs=4)
            slices = (zs_slices, zt_slices)[s][starts[c] // BANK]
            m0 = starts[c] % BANK
            nc.vector.tensor_copy(
                out=woven[c, s][:].rearrange("p (m t) -> p m t", t=PACK),
                in_=slices[:, :, m0 : m0 + CHUNKS[c]].rearrange("p t m -> p m t"),
            )

        def multiply(c, s):
            width = CHUNKS[c]
            codes = tile([P, width], U32, "z_codes", bufs=2 * len(CHUNKS))
            scales = tile([P, width], U8, "z_sc", bufs=2 * len(CHUNKS))
            nc.vector.quantize_mx(out=codes[:].bitcast(FP8X4), scales=scales[:], in_=woven[c, s][:])
            w_codes, w_sc = ((w3, w3_sc), (w4_codes, w4_sc))[s]
            for i in range(N // P // per_bank[c]):
                if s == 0:
                    accs[c, i] = bank((first_acc[c] + i) % BANKS, "acc%d_%d" % (c, i))
                for u in range(per_bank[c]):
                    n0 = (per_bank[c] * i + u) * P
                    nc.tensor.matmul_mx(
                        out=accs[c, i][:, u * width : (u + 1) * width],
                        lhsT=w_codes[:, n0 : n0 + P].bitcast(FP8X4), lhsT_scale=w_sc[:, n0 : n0 + P],
                        rhs=codes[:].bitcast(FP8X4), rhs_scale=scales[:],
                        start=(s == 0 and u == 0), stop=(s == 1 and u == per_bank[c] - 1),
                    )

        def store(c):
            width = CHUNKS[c]
            used = per_bank[c] * width
            for i in range(N // P // per_bank[c]):
                row = staging_rows[first_acc[c] + i][:, 0:used]
                if width < max(CHUNKS) and i == 1:
                    nc.vector.tensor_copy(out=row, in_=accs[c, i][:, 0:used])
                else:
                    nc.scalar.copy(out=row, in_=accs[c, i][:, 0:used])
                n0 = per_bank[c] * i * P
                block = out[n0 : n0 + per_bank[c] * P, starts[c] : starts[c] + width]
                nc.sync.dma_start(
                    out=block.rearrange("(u p) m -> p u m", u=per_bank[c]),
                    in_=row.rearrange("p (u m) -> p u m", u=per_bank[c]),
                )

        weave(0, 0)
        multiply(0, 0)
        for c in range(len(CHUNKS)):
            weave(c, 1)
            if c + 1 < len(CHUNKS):
                weave(c + 1, 0)
            multiply(c, 1)
            store(c)
            if c + 1 < len(CHUNKS):
                multiply(c + 1, 0)
